import numpy as np
import ml_dtypes


def mxq(x, axis, fmt="e4m3"):
    dtype, down = {"e4m3": (ml_dtypes.float8_e4m3fn, 7), "e5m2": (ml_dtypes.float8_e5m2, 14)}[fmt]
    v = np.moveaxis(np.asarray(x, np.float32).astype(ml_dtypes.bfloat16).astype(np.float64), axis, -1)
    blocks = v.reshape(v.shape[:-1] + (-1, 32))
    amax = np.abs(blocks).max(-1, keepdims=True)
    byte = np.maximum(np.where(amax > 0, np.frexp(amax)[1] - 1 + 127, 0) - down, 1)
    scale = np.exp2(byte - 127.0)
    codes = (blocks / scale).astype(np.float32).astype(dtype).astype(np.float64)
    return np.moveaxis((codes * scale).reshape(v.shape), -1, axis)


WIDE = False


def mx_kscale(k):
    if not WIDE:
        return np.ones(k)
    levels = np.array([10, -10, 5, -5, 0])
    if k % 512:
        return np.exp2(np.random.permutation(np.resize(levels, k // 32))).repeat(32)
    a = np.empty((k // 512, 16))
    for p in range(k // 512):
        a[p, :8] = np.random.permutation(np.resize(levels, 8))
        for g in range(8):
            far = levels[np.abs(levels - a[p, g]) >= 10]
            a[p, g + 8] = far[np.random.randint(len(far))]
    return np.exp2(a.ravel()).repeat(32)


def f64(x):
    return np.asarray(x).astype(np.float64)


def striped(idx):
    return np.tile(idx.reshape(-1, 16).T, (8, 1)).astype(np.uint16)


def unstriped(offs):
    return offs[:16].T.reshape(-1).astype(np.int64)


E2M1 = np.array([0.0, 0.5, 1.0, 1.5, 2.0, 3.0, 4.0, 6.0, -0.0, -0.5, -1.0, -1.5, -2.0, -3.0, -4.0, -6.0])


def pack_weight(w, fmt):
    k, n = w.shape
    w = f64(np.asarray(w, np.float32).astype(ml_dtypes.bfloat16)).reshape(k // 32, 32, n)
    amax = np.abs(w).max(1)
    if fmt == "e4m3":
        byte = np.frexp(amax)[1] - 1 + 127 - 7
    else:
        mant, ex = np.frexp(amax / 6.0)
        byte = np.where(mant > 0.5, ex, ex - 1) + 127
    byte = np.clip(np.where(amax > 0, byte, 1), 1, 254)
    scaled = (w * np.exp2(127.0 - byte)[:, None, :]).reshape(k, n).astype(np.float32)
    by_word = np.ascontiguousarray(scaled.reshape(k // 512, 128, 4, n).transpose(0, 1, 3, 2))
    if fmt == "e4m3":
        words = by_word.astype(ml_dtypes.float8_e4m3fn).view(np.uint8)
    else:
        c = by_word.astype(ml_dtypes.float4_e2m1fn).view(np.uint8) & 0xF
        words = (c[..., 0::2] | (c[..., 1::2] << 4)).reshape(k // 512, 128, 2 * n)
    return np.ascontiguousarray(words), np.ascontiguousarray(byte.astype(np.uint8).reshape(k // 512, 16, n))


def unpack_weight(words, scales, fmt):
    g, _, n = scales.shape
    words = np.ascontiguousarray(words).reshape(g, 128, n, -1)
    if fmt == "e4m3":
        vals = words.view(ml_dtypes.float8_e4m3fn).astype(np.float64)
    else:
        nib = np.empty((g, 128, n, 4), np.uint8)
        nib[..., 0::2] = words & 0xF
        nib[..., 1::2] = words >> 4
        vals = E2M1[nib]
    vals = vals * np.repeat(np.exp2(scales.astype(np.float64) - 127.0), 8, axis=1)[..., None]
    return vals.transpose(0, 1, 3, 2).reshape(g * 512, n)


def pack_table(v):
    words, scales = pack_weight(v, "e4m3")
    return np.concatenate([words.reshape(words.shape[0], -1), scales.reshape(scales.shape[0], -1)], axis=1)


def unpack_table(tab):
    g, t = tab.shape[0], tab.shape[1] // 528
    return unpack_weight(tab[:, :512 * t].reshape(g, 128, t, 4), tab[:, 512 * t:].reshape(g, 16, t), "e4m3")


K, M, T, S = 1024, 512, 512, 256


def setup_inputs():
    n = np.random.standard_normal
    s = mx_kscale(K)[:, None]
    return {
        "tab": pack_table(n((K, T)) * s),
        "w": (n((K, M)) / np.sqrt(K) / s).astype(np.float32),
        "wgo": np.tile(np.random.uniform(0.5, 2.0, S), (128, 1)).astype(np.float32),
        "offs": striped(np.random.permutation(T)[:S]),
        "offs2": striped(np.random.permutation(T)[:S]),
    }


def reference(tab, w, wgo, offs, offs2):
    tab_ = unpack_table(tab)[:, unstriped(offs)]
    w_ = mxq(f64(w), 0, "e4m3")
    y = w_.T @ tab_
    out = np.zeros((M, T))
    out[:, unstriped(offs2)] = f64(wgo)[0] * (y)
    return out

@@ -1,0 +1,125 @@
+from contextlib import ExitStack
+
+import concourse.mybir as mybir
+
+K, M, T, S = 1024, 512, 512, 256
+P = 128
+FLOPS = 2 * K * M * S
+
+F32 = mybir.dt.float32
+BF16 = mybir.dt.bfloat16
+I32 = mybir.dt.int32
+U32 = mybir.dt.uint32
+U16 = mybir.dt.uint16
+U8 = mybir.dt.uint8
+FP8X4 = mybir.dt.float8_e4m3fn_x4
+MULT = mybir.AluOpType.mult
+
+
+def interleave(copy, dst, src):
+    copy(
+        out=dst.rearrange("p (c i) j -> p c j i", i=4),
+        in_=src.rearrange("p j (c i) -> p c j i", i=4),
+    )
+
+
+def tile_list_tabscat_none_kernel(tc, tab, w, wgo, offs, offs2, out):
+    nc = tc.nc
+    w_view = w.rearrange("(a p j) n -> a p j n", a=2, j=4)
+    scale_rows = tab[:, 512 * T : 528 * T].rearrange("a (q t) -> a q t", t=T)
+
+    with ExitStack() as ctx:
+        keep = ctx.enter_context(tc.tile_pool(name="keep", bufs=1))
+        psum = ctx.enter_context(tc.psum_pool(name="psum", bufs=1))
+
+        list_in = keep.tile([P, S // 16], U16, name="list_in")
+        list_out = keep.tile([P, S // 16], U16, name="list_out")
+        tab_words = [keep.tile([P, T], I32, name=f"tab_words{a}") for a in range(2)]
+        tab_scales = keep.tile([P, T], U8, name="tab_scales", align_bytes=64)
+        g_words = [keep.tile([P, S], U32, name=f"g_words{a}", align_bytes=64) for a in range(2)]
+        g_scales = keep.tile([P, S], U8, name="g_scales", align_bytes=64)
+        weights = keep.tile([P, S], F32, name="weights")
+        raw_q = [[keep.tile([P, 4, P], F32, name=f"raw{m}_{a}") for a in range(2)] for m in range(2)]
+        raw_h = [keep.tile([P, 4, 2 * P], F32, name=f"rawh_{a}") for a in range(2)]
+        grouped = [keep.tile([P, 2, P, 4], BF16, name=f"grouped{m}", align_bytes=64) for m in range(4)]
+        w_codes = [keep.tile([P, 2 * P], U32, name=f"w_codes{m}", align_bytes=64) for m in range(4)]
+        w_scales = [keep.tile([P, 2 * P], U8, name=f"w_scales{m}", align_bytes=64) for m in range(4)]
+        y = [keep.tile([P, S], F32, name=f"y{m}") for m in range(4)]
+        placed = [keep.tile([P, T], F32, name=f"placed{m}") for m in range(4)]
+        acc = [psum.tile([P, S], F32, name=f"acc{m}") for m in range(4)]
+        warm = keep.tile([P, 1], F32, name="warm")
+        warm_out = keep.tile([P, 1], F32, name="warm_out")
+
+        nc.vector.memset(tab_scales[:].bitcast(I32), 0)
+        nc.sync.dma_start(list_in[:], offs)
+        for q in range(4):
+            nc.scalar.dma_start(
+                out=tab_scales[32 * q : 32 * q + 8, :].bitcast(I32),
+                in_=scale_rows[:, 4 * q : 4 * q + 4, :].bitcast(I32),
+            )
+        for a in range(2):
+            nc.sync.dma_start(
+                out=tab_words[a][:],
+                in_=tab[a, 0 : 512 * T].rearrange("(p t) -> p t", p=P).bitcast(I32),
+            )
+        nc.sync.dma_start(out=raw_q[0][0][:], in_=w_view[0, :, :, 0:P])
+        nc.gpsimd.dma_start(out=raw_q[0][1][:], in_=w_view[1, :, :, 0:P])
+        nc.gpsimd.dma_start(out=weights[:], in_=wgo)
+        nc.sync.dma_start(out=raw_q[1][0][:], in_=w_view[0, :, :, P : 2 * P])
+        nc.sync.dma_start(out=raw_q[1][1][:], in_=w_view[1, :, :, P : 2 * P])
+        nc.sync.dma_start(list_out[:], offs2)
+        for a in range(2):
+            nc.sync.dma_start(out=raw_h[a][:], in_=w_view[a, :, :, 2 * P : 4 * P])
+
+        nc.vector.memset(warm[:], 0.0)
+        nc.scalar.copy(out=warm_out[:], in_=warm[:])
+        for m in range(4):
+            nc.vector.memset(placed[m][:], 0.0)
+
+        for a in range(2):
+            nc.vector.tensor_copy(g_words[a][:], tab_words[a][:].bitcast(U32).indirect(list_in[:]))
+        nc.vector.tensor_copy(g_scales[:], tab_scales[:].indirect(list_in[:]))
+
+        def raw(m, a):
+            return raw_q[m][a][:] if m < 2 else raw_h[a][:, :, (m - 2) * P : (m - 1) * P]
+
+        def prepare(m):
+            for a in range(2):
+                copy = nc.vector.tensor_copy if (m == 0 and a == 1) else nc.scalar.copy
+                interleave(copy, grouped[m][:, a, :, :], raw(m, a))
+            nc.vector.quantize_mx(
+                out=w_codes[m][:].bitcast(FP8X4),
+                scales=w_scales[m][:],
+                in_=grouped[m][:].rearrange("p a c j -> p (a c j)"),
+            )
+
+        def multiply(m):
+            for a in range(2):
+                cols = slice(a * P, (a + 1) * P)
+                nc.tensor.matmul_mx(
+                    out=acc[m][:],
+                    lhsT=w_codes[m][:, cols].bitcast(FP8X4),
+                    lhsT_scale=w_scales[m][:, cols],
+                    rhs=g_words[a][:].bitcast(FP8X4),
+                    rhs_scale=g_scales[4 * a : P, :],
+                    start=(a == 0),
+                    stop=(a == 1),
+                )
+            nc.scalar.copy(out=y[m][:], in_=acc[m][:])
+
+        def place(m):
+            nc.vector.tensor_tensor(placed[m][:].indirect(list_out[:]), y[m][:], weights[:], MULT)
+            nc.sync.dma_start(out=out[m * P : (m + 1) * P, :], in_=placed[m][:])
+
+        prepare(0)
+        multiply(0)
+        prepare(1)
+        place(0)
+        multiply(1)
+        prepare(2)
+        place(1)
+        multiply(2)
+        prepare(3)
+        place(2)
+        multiply(3)
+        place(3)

@@ -34,92 +34,129 @@ def tile_list_tabscat_none_kernel(tc, tab, w, wgo, offs, offs2, out):
 
         list_in = keep.tile([P, S // 16], U16, name="list_in")
         list_out = keep.tile([P, S // 16], U16, name="list_out")
-        tab_words = [keep.tile([P, T], I32, name=f"tab_words{a}") for a in range(2)]
+        tab_words_all = keep.tile([P, 2, T], I32, name="tab_words_all")
+        tab_words = [tab_words_all[:, a, :] for a in range(2)]
         tab_scales = keep.tile([P, T], U8, name="tab_scales", align_bytes=64)
         g_words = [keep.tile([P, S], U32, name=f"g_words{a}", align_bytes=64) for a in range(2)]
         g_scales = keep.tile([P, S], U8, name="g_scales", align_bytes=64)
         weights = keep.tile([P, S], F32, name="weights")
-        raw_q = [[keep.tile([P, 4, P], F32, name=f"raw{m}_{a}") for a in range(2)] for m in range(2)]
-        raw_h = [keep.tile([P, 4, 2 * P], F32, name=f"rawh_{a}") for a in range(2)]
+        raw = [[keep.tile([P, 4, 2 * P], F32, name=f"raw{h}_{a}") for a in range(2)] for h in range(2)]
         grouped = [keep.tile([P, 2, P, 4], BF16, name=f"grouped{m}", align_bytes=64) for m in range(4)]
         w_codes = [keep.tile([P, 2 * P], U32, name=f"w_codes{m}", align_bytes=64) for m in range(4)]
         w_scales = [keep.tile([P, 2 * P], U8, name=f"w_scales{m}", align_bytes=64) for m in range(4)]
-        y = [keep.tile([P, S], F32, name=f"y{m}") for m in range(4)]
         placed = [keep.tile([P, T], F32, name=f"placed{m}") for m in range(4)]
-        acc = [psum.tile([P, S], F32, name=f"acc{m}") for m in range(4)]
         warm = keep.tile([P, 1], F32, name="warm")
         warm_out = keep.tile([P, 1], F32, name="warm_out")
 
         nc.vector.memset(tab_scales[:].bitcast(I32), 0)
         nc.sync.dma_start(list_in[:], offs)
+        nc.sync.dma_start(
+            out=tab_words_all[:],
+            in_=tab[:, 0 : 512 * T].rearrange("a (p t) -> p a t", p=P).bitcast(I32),
+        )
         for q in range(4):
-            nc.scalar.dma_start(
+            nc.sync.dma_start(
                 out=tab_scales[32 * q : 32 * q + 8, :].bitcast(I32),
                 in_=scale_rows[:, 4 * q : 4 * q + 4, :].bitcast(I32),
             )
-        for a in range(2):
+
+        def load_w(half, a):
             nc.sync.dma_start(
-                out=tab_words[a][:],
-                in_=tab[a, 0 : 512 * T].rearrange("(p t) -> p t", p=P).bitcast(I32),
+                out=raw[half][a][:], in_=w_view[a, :, :, half * 2 * P : (half + 1) * 2 * P]
             )
-        nc.sync.dma_start(out=raw_q[0][0][:], in_=w_view[0, :, :, 0:P])
-        nc.gpsimd.dma_start(out=raw_q[0][1][:], in_=w_view[1, :, :, 0:P])
-        nc.gpsimd.dma_start(out=weights[:], in_=wgo)
-        nc.sync.dma_start(out=raw_q[1][0][:], in_=w_view[0, :, :, P : 2 * P])
-        nc.sync.dma_start(out=raw_q[1][1][:], in_=w_view[1, :, :, P : 2 * P])
+
+        load_w(0, 0)
+        load_w(0, 1)
+        nc.sync.dma_start(out=weights[:], in_=wgo)
         nc.sync.dma_start(list_out[:], offs2)
-        for a in range(2):
-            nc.sync.dma_start(out=raw_h[a][:], in_=w_view[a, :, :, 2 * P : 4 * P])
+        load_w(1, 0)
+        load_w(1, 1)
 
         nc.vector.memset(warm[:], 0.0)
         nc.scalar.copy(out=warm_out[:], in_=warm[:])
         for m in range(4):
             nc.vector.memset(placed[m][:], 0.0)
 
-        for a in range(2):
-            nc.vector.tensor_copy(g_words[a][:], tab_words[a][:].bitcast(U32).indirect(list_in[:]))
-        nc.vector.tensor_copy(g_scales[:], tab_scales[:].indirect(list_in[:]))
+        def regroup(copy, m, a, c0=0, c1=P):
+            interleave(copy, grouped[m][:, a, c0:c1, :], raw[m // 2][a][:, :, m % 2 * P + c0 : m % 2 * P + c1])
 
-        def raw(m, a):
-            return raw_q[m][a][:] if m < 2 else raw_h[a][:, :, (m - 2) * P : (m - 1) * P]
-
-        def prepare(m):
-            for a in range(2):
-                copy = nc.vector.tensor_copy if (m == 0 and a == 1) else nc.scalar.copy
-                interleave(copy, grouped[m][:, a, :, :], raw(m, a))
+        def quantize(m, a0, a1):
             nc.vector.quantize_mx(
-                out=w_codes[m][:].bitcast(FP8X4),
-                scales=w_scales[m][:],
-                in_=grouped[m][:].rearrange("p a c j -> p (a c j)"),
+                out=w_codes[m][:, a0 * P : a1 * P].bitcast(FP8X4),
+                scales=w_scales[m][:, a0 * P : a1 * P],
+                in_=grouped[m][:, a0:a1, :, :].rearrange("p a c j -> p (a c j)"),
             )
 
-        def multiply(m):
+        def gather_words(a):
+            nc.vector.tensor_copy(
+                g_words[a][:],
+                tab_words[a].bitcast(U32).indirect(list_in[:]),
+            )
+
+        def gather_scales():
+            nc.vector.tensor_copy(
+                g_scales[:],
+                tab_scales[:].indirect(list_in[:]),
+            )
+
+        def multiply(m, acc, j0, j1):
             for a in range(2):
                 cols = slice(a * P, (a + 1) * P)
                 nc.tensor.matmul_mx(
-                    out=acc[m][:],
+                    out=acc[:],
                     lhsT=w_codes[m][:, cols].bitcast(FP8X4),
                     lhsT_scale=w_scales[m][:, cols],
-                    rhs=g_words[a][:].bitcast(FP8X4),
-                    rhs_scale=g_scales[4 * a : P, :],
+                    rhs=g_words[a][:, j0:j1].bitcast(FP8X4),
+                    rhs_scale=g_scales[4 * a : P, j0:j1],
                     start=(a == 0),
                     stop=(a == 1),
                 )
-            nc.scalar.copy(out=y[m][:], in_=acc[m][:])
 
-        def place(m):
-            nc.vector.tensor_tensor(placed[m][:].indirect(list_out[:]), y[m][:], weights[:], MULT)
+        def place(m, y, j0, j1):
+            nc.vector.tensor_tensor(
+                placed[m][:].indirect(list_out[:, j0 // 16 : j1 // 16]), y[:, j0:j1], weights[:, j0:j1], MULT
+            )
+
+        def store(m):
             nc.sync.dma_start(out=out[m * P : (m + 1) * P, :], in_=placed[m][:])
 
-        prepare(0)
-        multiply(0)
-        prepare(1)
-        place(0)
-        multiply(1)
-        prepare(2)
-        place(1)
-        multiply(2)
-        prepare(3)
-        place(2)
-        multiply(3)
-        place(3)
+        def copy_out(m, acc):
+            y = keep.tile([P, S], F32, name=f"y{m}")
+            nc.scalar.copy(out=y[:], in_=acc[:])
+            return y
+
+        acc = [psum.tile([P, S], F32, name=f"acc{m}") for m in range(4)]
+
+        gather_words(0)
+        gather_words(1)
+        gather_scales()
+        regroup(nc.scalar.copy, 0, 0)
+        quantize(0, 0, 1)
+        regroup(nc.scalar.copy, 1, 0)
+        regroup(nc.vector.tensor_copy, 0, 1)
+        quantize(0, 1, 2)
+        multiply(0, acc[0], 0, S)
+        regroup(nc.scalar.copy, 1, 1)
+        quantize(1, 0, 2)
+        y0 = copy_out(0, acc[0])
+        multiply(1, acc[1], 0, S)
+        place(0, y0, 0, S)
+        store(0)
+        y1 = copy_out(1, acc[1])
+        regroup(nc.scalar.copy, 2, 0)
+        regroup(nc.scalar.copy, 2, 1)
+        place(1, y1, 0, P)
+        quantize(2, 0, 2)
+        multiply(2, acc[2], 0, S)
+        place(1, y1, P, S)
+        store(1)
+        regroup(nc.scalar.copy, 3, 0)
+        y2 = copy_out(2, acc[2])
+        regroup(nc.scalar.copy, 3, 1)
+        quantize(3, 0, 2)
+        multiply(3, acc[3], 0, S)
+        place(2, y2, 0, S)
+        store(2)
+        y3 = copy_out(3, acc[3])
+        place(3, y3, 0, S)
+        store(3)

@@ -40,7 +40,13 @@ def tile_list_tabscat_none_kernel(tc, tab, w, wgo, offs, offs2, out):
         g_words = [keep.tile([P, S], U32, name=f"g_words{a}", align_bytes=64) for a in range(2)]
         g_scales = keep.tile([P, S], U8, name="g_scales", align_bytes=64)
         weights = keep.tile([P, S], F32, name="weights")
-        raw = [[keep.tile([P, 4, 2 * P], F32, name=f"raw{h}_{a}") for a in range(2)] for h in range(2)]
+        raw_pair = [keep.tile([P, 4, 2 * P], F32, name=f"raw01_{a}") for a in range(2)]
+        raw = [[raw_pair[a][:, :, m * P : (m + 1) * P] for a in range(2)] for m in range(2)]
+        for m in (2, 3):
+            raw.append([])
+            for a in range(2):
+                piece = keep.tile([P, 4, P], F32, name=f"raw{m}_{a}", tag=f"raw{m}_{a}")
+                raw[m].append(piece[:])
         grouped = [keep.tile([P, 2, P, 4], BF16, name=f"grouped{m}", align_bytes=64) for m in range(4)]
         w_codes = [keep.tile([P, 2 * P], U32, name=f"w_codes{m}", align_bytes=64) for m in range(4)]
         w_scales = [keep.tile([P, 2 * P], U8, name=f"w_scales{m}", align_bytes=64) for m in range(4)]
@@ -60,17 +66,19 @@ def tile_list_tabscat_none_kernel(tc, tab, w, wgo, offs, offs2, out):
                 in_=scale_rows[:, 4 * q : 4 * q + 4, :].bitcast(I32),
             )
 
-        def load_w(half, a):
-            nc.sync.dma_start(
-                out=raw[half][a][:], in_=w_view[a, :, :, half * 2 * P : (half + 1) * 2 * P]
-            )
+        def load_pair(a):
+            nc.sync.dma_start(out=raw_pair[a][:], in_=w_view[a, :, :, 0 : 2 * P])
 
-        load_w(0, 0)
-        load_w(0, 1)
+        def load_w(m, a):
+            nc.sync.dma_start(out=raw[m][a], in_=w_view[a, :, :, m * P : (m + 1) * P])
+
+        load_pair(0)
+        load_pair(1)
         nc.sync.dma_start(out=weights[:], in_=wgo)
         nc.sync.dma_start(list_out[:], offs2)
-        load_w(1, 0)
-        load_w(1, 1)
+        for m in (2, 3):
+            for a in range(2):
+                load_w(m, a)
 
         nc.vector.memset(warm[:], 0.0)
         nc.scalar.copy(out=warm_out[:], in_=warm[:])
@@ -78,7 +86,7 @@ def tile_list_tabscat_none_kernel(tc, tab, w, wgo, offs, offs2, out):
             nc.vector.memset(placed[m][:], 0.0)
 
         def regroup(copy, m, a, c0=0, c1=P):
-            interleave(copy, grouped[m][:, a, c0:c1, :], raw[m // 2][a][:, :, m % 2 * P + c0 : m % 2 * P + c1])
+            interleave(copy, grouped[m][:, a, c0:c1, :], raw[m][a][:, :, c0:c1])
 
         def quantize(m, a0, a1):
             nc.vector.quantize_mx(
@@ -120,8 +128,8 @@ def tile_list_tabscat_none_kernel(tc, tab, w, wgo, offs, offs2, out):
         def store(m):
             nc.sync.dma_start(out=out[m * P : (m + 1) * P, :], in_=placed[m][:])
 
-        def copy_out(m, acc):
-            y = keep.tile([P, S], F32, name=f"y{m}")
+        def copy_out(m, acc, tag):
+            y = keep.tile([P, S], F32, name=f"y{m}", tag=tag)
             nc.scalar.copy(out=y[:], in_=acc[:])
             return y
 
@@ -137,26 +145,25 @@ def tile_list_tabscat_none_kernel(tc, tab, w, wgo, offs, offs2, out):
         quantize(0, 1, 2)
         multiply(0, acc[0], 0, S)
         regroup(nc.scalar.copy, 1, 1)
+        y0 = copy_out(0, acc[0], "y0")
         quantize(1, 0, 2)
-        y0 = copy_out(0, acc[0])
         multiply(1, acc[1], 0, S)
         place(0, y0, 0, S)
         store(0)
-        y1 = copy_out(1, acc[1])
         regroup(nc.scalar.copy, 2, 0)
         regroup(nc.scalar.copy, 2, 1)
-        place(1, y1, 0, P)
         quantize(2, 0, 2)
+        y1 = copy_out(1, acc[1], "raw2_1")
         multiply(2, acc[2], 0, S)
-        place(1, y1, P, S)
+        place(1, y1, 0, S)
         store(1)
         regroup(nc.scalar.copy, 3, 0)
-        y2 = copy_out(2, acc[2])
         regroup(nc.scalar.copy, 3, 1)
         quantize(3, 0, 2)
+        y2 = copy_out(2, acc[2], "raw3_1")
         multiply(3, acc[3], 0, S)
         place(2, y2, 0, S)
         store(2)
-        y3 = copy_out(3, acc[3])
+        y3 = copy_out(3, acc[3], "y3")
         place(3, y3, 0, S)
         store(3)

from contextlib import ExitStack

import concourse.mybir as mybir

K, M, T, S = 1024, 512, 512, 256
P = 128
FLOPS = 2 * K * M * S

F32 = mybir.dt.float32
BF16 = mybir.dt.bfloat16
I32 = mybir.dt.int32
U32 = mybir.dt.uint32
U16 = mybir.dt.uint16
U8 = mybir.dt.uint8
FP8X4 = mybir.dt.float8_e4m3fn_x4
MULT = mybir.AluOpType.mult


def interleave(copy, dst, src):
    copy(
        out=dst.rearrange("p (c i) j -> p c j i", i=4),
        in_=src.rearrange("p j (c i) -> p c j i", i=4),
    )


def tile_list_tabscat_none_kernel(tc, tab, w, wgo, offs, offs2, out):
    nc = tc.nc
    w_view = w.rearrange("(a p j) n -> a p j n", a=2, j=4)
    scale_rows = tab[:, 512 * T : 528 * T].rearrange("a (q t) -> a q t", t=T)

    with ExitStack() as ctx:
        keep = ctx.enter_context(tc.tile_pool(name="keep", bufs=1))
        psum = ctx.enter_context(tc.psum_pool(name="psum", bufs=1))

        list_in = keep.tile([P, S // 16], U16, name="list_in")
        list_out = keep.tile([P, S // 16], U16, name="list_out")
        tab_words_all = keep.tile([P, 2, T], I32, name="tab_words_all")
        tab_words = [tab_words_all[:, a, :] for a in range(2)]
        tab_scales = keep.tile([P, T], U8, name="tab_scales", align_bytes=64)
        g_words = [keep.tile([P, S], U32, name=f"g_words{a}", align_bytes=64) for a in range(2)]
        g_scales = keep.tile([P, S], U8, name="g_scales", align_bytes=64)
        weights = keep.tile([P, S], F32, name="weights")
        raw_pair = [keep.tile([P, 4, 2 * P], F32, name=f"raw01_{a}") for a in range(2)]
        raw = [[raw_pair[a][:, :, m * P : (m + 1) * P] for a in range(2)] for m in range(2)]
        for m in (2, 3):
            raw.append([])
            for a in range(2):
                piece = keep.tile([P, 4, P], F32, name=f"raw{m}_{a}", tag=f"raw{m}_{a}")
                raw[m].append(piece[:])
        grouped = [keep.tile([P, 2, P, 4], BF16, name=f"grouped{m}", align_bytes=64) for m in range(4)]
        w_codes = [keep.tile([P, 2 * P], U32, name=f"w_codes{m}", align_bytes=64) for m in range(4)]
        w_scales = [keep.tile([P, 2 * P], U8, name=f"w_scales{m}", align_bytes=64) for m in range(4)]
        placed = [keep.tile([P, T], F32, name=f"placed{m}") for m in range(4)]
        warm = keep.tile([P, 1], F32, name="warm")
        warm_out = keep.tile([P, 1], F32, name="warm_out")

        nc.vector.memset(tab_scales[:].bitcast(I32), 0)
        nc.sync.dma_start(list_in[:], offs)
        nc.sync.dma_start(
            out=tab_words_all[:],
            in_=tab[:, 0 : 512 * T].rearrange("a (p t) -> p a t", p=P).bitcast(I32),
        )
        for q in range(4):
            nc.sync.dma_start(
                out=tab_scales[32 * q : 32 * q + 8, :].bitcast(I32),
                in_=scale_rows[:, 4 * q : 4 * q + 4, :].bitcast(I32),
            )

        def load_pair(a):
            nc.sync.dma_start(out=raw_pair[a][:], in_=w_view[a, :, :, 0 : 2 * P])

        def load_w(m, a):
            nc.sync.dma_start(out=raw[m][a], in_=w_view[a, :, :, m * P : (m + 1) * P])

        load_pair(0)
        load_pair(1)
        nc.sync.dma_start(out=weights[:], in_=wgo)
        nc.sync.dma_start(list_out[:], offs2)
        for m in (2, 3):
            for a in range(2):
                load_w(m, a)

        nc.vector.memset(warm[:], 0.0)
        nc.scalar.copy(out=warm_out[:], in_=warm[:])
        for m in range(4):
            nc.vector.memset(placed[m][:], 0.0)

        def regroup(copy, m, a, c0=0, c1=P):
            interleave(copy, grouped[m][:, a, c0:c1, :], raw[m][a][:, :, c0:c1])

        def quantize(m, a0, a1):
            nc.vector.quantize_mx(
                out=w_codes[m][:, a0 * P : a1 * P].bitcast(FP8X4),
                scales=w_scales[m][:, a0 * P : a1 * P],
                in_=grouped[m][:, a0:a1, :, :].rearrange("p a c j -> p (a c j)"),
            )

        def gather_words(a):
            nc.vector.tensor_copy(
                g_words[a][:],
                tab_words[a].bitcast(U32).indirect(list_in[:]),
            )

        def gather_scales():
            nc.vector.tensor_copy(
                g_scales[:],
                tab_scales[:].indirect(list_in[:]),
            )

        def multiply(m, acc, j0, j1):
            for a in range(2):
                cols = slice(a * P, (a + 1) * P)
                nc.tensor.matmul_mx(
                    out=acc[:],
                    lhsT=w_codes[m][:, cols].bitcast(FP8X4),
                    lhsT_scale=w_scales[m][:, cols],
                    rhs=g_words[a][:, j0:j1].bitcast(FP8X4),
                    rhs_scale=g_scales[4 * a : P, j0:j1],
                    start=(a == 0),
                    stop=(a == 1),
                )

        def place(m, y, j0, j1):
            nc.vector.tensor_tensor(
                placed[m][:].indirect(list_out[:, j0 // 16 : j1 // 16]), y[:, j0:j1], weights[:, j0:j1], MULT
            )

        def store(m):
            nc.sync.dma_start(out=out[m * P : (m + 1) * P, :], in_=placed[m][:])

        def copy_out(m, acc, tag):
            y = keep.tile([P, S], F32, name=f"y{m}", tag=tag)
            nc.scalar.copy(out=y[:], in_=acc[:])
            return y

        acc = [psum.tile([P, S], F32, name=f"acc{m}") for m in range(4)]

        gather_words(0)
        gather_words(1)
        gather_scales()
        regroup(nc.scalar.copy, 0, 0)
        quantize(0, 0, 1)
        regroup(nc.scalar.copy, 1, 0)
        regroup(nc.vector.tensor_copy, 0, 1)
        quantize(0, 1, 2)
        multiply(0, acc[0], 0, S)
        regroup(nc.scalar.copy, 1, 1)
        y0 = copy_out(0, acc[0], "y0")
        quantize(1, 0, 2)
        multiply(1, acc[1], 0, S)
        place(0, y0, 0, S)
        store(0)
        regroup(nc.scalar.copy, 2, 0)
        regroup(nc.scalar.copy, 2, 1)
        quantize(2, 0, 2)
        y1 = copy_out(1, acc[1], "raw2_1")
        multiply(2, acc[2], 0, S)
        place(1, y1, 0, S)
        store(1)
        regroup(nc.scalar.copy, 3, 0)
        regroup(nc.scalar.copy, 3, 1)
        quantize(3, 0, 2)
        y2 = copy_out(2, acc[2], "raw3_1")
        multiply(3, acc[3], 0, S)
        place(2, y2, 0, S)
        store(2)
        y3 = copy_out(3, acc[3], "y3")
        place(3, y3, 0, S)
        store(3)
